import numpy as np
import ml_dtypes


def mxq(x, axis, fmt="e4m3"):
    dtype, down = {"e4m3": (ml_dtypes.float8_e4m3fn, 7), "e5m2": (ml_dtypes.float8_e5m2, 14)}[fmt]
    v = np.moveaxis(np.asarray(x, np.float32).astype(ml_dtypes.bfloat16).astype(np.float64), axis, -1)
    blocks = v.reshape(v.shape[:-1] + (-1, 32))
    amax = np.abs(blocks).max(-1, keepdims=True)
    byte = np.maximum(np.where(amax > 0, np.frexp(amax)[1] - 1 + 127, 0) - down, 1)
    scale = np.exp2(byte - 127.0)
    codes = (blocks / scale).astype(np.float32).astype(dtype).astype(np.float64)
    return np.moveaxis((codes * scale).reshape(v.shape), -1, axis)


WIDE = False


def mx_kscale(k):
    if not WIDE:
        return np.ones(k)
    levels = np.array([10, -10, 5, -5, 0])
    if k % 512:
        return np.exp2(np.random.permutation(np.resize(levels, k // 32))).repeat(32)
    a = np.empty((k // 512, 16))
    for p in range(k // 512):
        a[p, :8] = np.random.permutation(np.resize(levels, 8))
        for g in range(8):
            far = levels[np.abs(levels - a[p, g]) >= 10]
            a[p, g + 8] = far[np.random.randint(len(far))]
    return np.exp2(a.ravel()).repeat(32)


def f64(x):
    return np.asarray(x).astype(np.float64)


def striped8(idx):
    return np.asarray(idx).reshape(8, -1, 16).transpose(0, 2, 1).reshape(128, -1).astype(np.uint16)


def unstriped8(offs):
    return offs.reshape(8, 16, -1).transpose(0, 2, 1).reshape(8, -1).astype(np.int64)


def pick8(x, idx, run):
    r = np.arange(len(x))
    return x[r[:, None], idx[r % (8 * run) // run]]


E2M1 = np.array([0.0, 0.5, 1.0, 1.5, 2.0, 3.0, 4.0, 6.0, -0.0, -0.5, -1.0, -1.5, -2.0, -3.0, -4.0, -6.0])


def pack_weight(w, fmt):
    k, n = w.shape
    w = f64(np.asarray(w, np.float32).astype(ml_dtypes.bfloat16)).reshape(k // 32, 32, n)
    amax = np.abs(w).max(1)
    if fmt == "e4m3":
        byte = np.frexp(amax)[1] - 1 + 127 - 7
    else:
        mant, ex = np.frexp(amax / 6.0)
        byte = np.where(mant > 0.5, ex, ex - 1) + 127
    byte = np.clip(np.where(amax > 0, byte, 1), 1, 254)
    scaled = (w * np.exp2(127.0 - byte)[:, None, :]).reshape(k, n).astype(np.float32)
    by_word = np.ascontiguousarray(scaled.reshape(k // 512, 128, 4, n).transpose(0, 1, 3, 2))
    if fmt == "e4m3":
        words = by_word.astype(ml_dtypes.float8_e4m3fn).view(np.uint8)
    else:
        c = by_word.astype(ml_dtypes.float4_e2m1fn).view(np.uint8) & 0xF
        words = (c[..., 0::2] | (c[..., 1::2] << 4)).reshape(k // 512, 128, 2 * n)
    return np.ascontiguousarray(words), np.ascontiguousarray(byte.astype(np.uint8).reshape(k // 512, 16, n))


def unpack_weight(words, scales, fmt):
    g, _, n = scales.shape
    words = np.ascontiguousarray(words).reshape(g, 128, n, -1)
    if fmt == "e4m3":
        vals = words.view(ml_dtypes.float8_e4m3fn).astype(np.float64)
    else:
        nib = np.empty((g, 128, n, 4), np.uint8)
        nib[..., 0::2] = words & 0xF
        nib[..., 1::2] = words >> 4
        vals = E2M1[nib]
    vals = vals * np.repeat(np.exp2(scales.astype(np.float64) - 127.0), 8, axis=1)[..., None]
    return vals.transpose(0, 1, 3, 2).reshape(g * 512, n)


def softplus(v):
    return np.log(1.0 + np.exp(v))


D, T, I, Q = 512, 1024, 512, 128


def setup_inputs():
    n = np.random.standard_normal
    idx = np.stack([np.random.permutation(T)[:I] for _ in range(8)])
    idx2 = np.stack([np.random.permutation(T)[:I] for _ in range(8)])
    idx3 = np.stack([np.random.permutation(T)[:I] for _ in range(8)])
    idx4 = np.stack([np.random.permutation(T)[:I] for _ in range(8)])
    fd = mx_kscale(D)
    keysp = pack_weight(n((D, T)) / fd[:, None], "e2m1")
    return {
        "query": (n((D, Q)) * 0.9 / np.sqrt(D) * fd[:, None]).astype(np.float32),
        "query2": (n((D, Q)) * 0.9 / np.sqrt(D) * fd[:, None]).astype(np.float32),
        "keys_words": keysp[0],
        "keys_scales": keysp[1],
        "lam": (np.random.uniform(0.6, 1.2, (Q, 1))).astype(np.float32),
        "old": (1.0 * n((Q, T))).astype(np.float32),
        "offs": striped8(idx),
        "offs2": striped8(idx2),
        "offs3": striped8(idx3),
        "offs4": striped8(idx4),
    }


def reference(query, query2, keys_words, keys_scales, lam, old, offs, offs2, offs3, offs4):
    idx = unstriped8(offs)
    idx2 = unstriped8(offs2)
    idx3 = unstriped8(offs3)
    idx4 = unstriped8(offs4)
    keysu = unpack_weight(keys_words, keys_scales, "e2m1")
    queryq = mxq(f64(query), 0, "e4m3")
    a = queryq.T @ keysu
    query2q = mxq(f64(query2), 0, "e4m3")
    b = query2q.T @ keysu
    w = pick8(a, idx, 16) / (softplus(pick8(b, idx2, 16)) + 0.5) * f64(lam)
    f1 = np.zeros((Q, T))
    f1[np.arange(Q)[:, None], idx[np.arange(Q) % 128 // 16]] = w
    f2 = f1 + f64(old)
    y = np.maximum(pick8(f2, idx3, 16), pick8(f2, idx4, 16))
    return y

@@ -1,0 +1,184 @@
+import math
+from contextlib import ExitStack
+
+import concourse.mybir as mybir
+
+
+D, T, I, Q = 512, 1024, 512, 128
+FLOPS = 2 * 2 * D * T * Q
+
+F32 = mybir.dt.float32
+BF16 = mybir.dt.bfloat16
+I32 = mybir.dt.int32
+U32 = mybir.dt.uint32
+U16 = mybir.dt.uint16
+U8 = mybir.dt.uint8
+FP8X4 = mybir.dt.float8_e4m3fn_x4
+FP4X4 = mybir.dt.float4_e2m1fn_x4
+ALU = mybir.AluOpType
+ACT = mybir.ActivationFunctionType
+
+P = 128
+PACK = 4
+CLAMP = 41.5
+ROOT_E = math.exp(0.5)
+
+
+def entries(offsets, first, last):
+    return offsets[:, first // 16 : last // 16]
+
+
+def tile_attend_worthfor_lean_throughtwo_heads_kernel(
+    tc, query, query2, keys_words, keys_scales, lam, old, offs, offs2, offs3, offs4, out
+):
+    nc = tc.nc
+    with ExitStack() as ctx:
+        lists = ctx.enter_context(tc.tile_pool(name="lists", bufs=1))
+        sb = ctx.enter_context(tc.tile_pool(name="sb", bufs=1))
+        psum = ctx.enter_context(tc.psum_pool(name="psum", bufs=1))
+
+        q2_raw = sb.tile([P, PACK, Q], F32, tag="q2_then_old")
+        nc.sync.dma_start(q2_raw[:], query2.rearrange("(p j) q -> p j q", j=PACK))
+        key_scales = sb.tile([P, T], U8, align_bytes=64)
+
+        for quad in range(4):
+            nc.scalar.dma_start(
+                key_scales[32 * quad : 32 * quad + 4, :].bitcast(I32),
+                keys_scales[0, 4 * quad : 4 * quad + 4, :].bitcast(I32),
+            )
+        key_words = sb.tile([P, 2 * T], U8, align_bytes=64)
+        nc.sync.dma_start(key_words[:].bitcast(I32), keys_words[0].bitcast(I32))
+        q_raw = sb.tile([P, PACK, Q], F32)
+        nc.sync.dma_start(q_raw[:], query.rearrange("(p j) q -> p j q", j=PACK))
+        idx2 = lists.tile([P, I // 16], U16)
+        nc.sync.dma_start(idx2[:], offs2)
+        lam_col = sb.tile([P, 1], F32)
+        nc.gpsimd.dma_start(lam_col[:], lam)
+        idx = lists.tile([P, I // 16], U16)
+        nc.sync.dma_start(idx[:], offs)
+
+        one = sb.tile([P, 1], F32)
+        nc.vector.memset(one[:], 1.0)
+        root_e = sb.tile([P, 1], F32)
+        nc.scalar.activation(root_e[:], one[:], ACT.Copy, scale=ROOT_E)
+        minus_half = sb.tile([P, 1], F32)
+        nc.vector.memset(minus_half[:], -0.5)
+        f1 = sb.tile([P, T], F32)
+        nc.vector.memset(f1[:], 0.0)
+
+        def interleave(raw, name):
+            grouped = sb.tile([P, Q, PACK], BF16, align_bytes=64, name=name + "_grouped")
+            nc.vector.tensor_copy(out=grouped[:], in_=raw[:].rearrange("p j q -> p q j"))
+            return grouped
+
+        def quantise(grouped, name):
+            codes = sb.tile([P, Q], U32, align_bytes=64, name=name + "_codes", tag="codes")
+            scales = sb.tile([P, Q], U8, align_bytes=64, name=name + "_scales", tag="scales")
+            nc.vector.quantize_mx(
+                out=codes[:].bitcast(FP8X4), scales=scales[:], in_=grouped[:].rearrange("p q j -> p (q j)")
+            )
+            return codes, scales
+
+        def scores(codes, scales, first, last, name):
+            bank = psum.tile([P, last - first], F32, name=name)
+            nc.tensor.matmul_mx(
+                out=bank[:],
+                lhsT=codes[:].bitcast(FP8X4),
+                lhsT_scale=scales[:],
+                rhs=key_words[:, 2 * first : 2 * last].bitcast(FP4X4),
+                rhs_scale=key_scales[:, first:last],
+                start=True,
+                stop=True,
+            )
+            return bank
+
+        q2_codes, q2_scales = quantise(interleave(q2_raw, "q2"), "q2")
+        q_grouped = interleave(q_raw, "q")
+
+
+        old_sb = sb.tile([P, T], F32, tag="q2_then_old")
+        nc.sync.dma_start(old_sb[:], old)
+        idx3 = lists.tile([P, I // 16], U16)
+        nc.sync.dma_start(idx3[:], offs3)
+        idx4 = lists.tile([P, I // 16], U16)
+        nc.sync.dma_start(idx4[:], offs4)
+
+        b_sb = sb.tile([P, T], F32)
+        for n in range(4):
+            first, last = 256 * n, 256 * (n + 1)
+            bank = scores(q2_codes, q2_scales, first, last, "b_bank%d" % n)
+            if n % 2:
+                nc.vector.tensor_copy(out=b_sb[:, first:last], in_=bank[:])
+            else:
+                nc.scalar.copy(out=b_sb[:, first:last], in_=bank[:])
+
+        q_codes, q_scales = quantise(q_grouped, "q")
+        e = sb.tile([P, I], F32)
+        g = sb.tile([P, I], F32)
+        work = sb.tile([P, 448], F32)
+        ag_head = sb.tile([P, 128], F32)
+        lam_rows = sb.tile([P, 128], F32)
+        nc.scalar.copy(out=lam_rows[:], in_=lam_col[:].to_broadcast([P, 128]))
+        nc.scalar.copy(out=work[:, 0:128], in_=lam_col[:].to_broadcast([P, 128]))
+        e_head = work[:, 256:384]
+        nc.scalar.activation(e[:, 256:512], b_sb[:].indirect(entries(idx2, 256, 512)), ACT.Exp)
+        for first in (0, 256):
+            last = first + 256
+            nc.vector.tensor_scalar(
+                g[:, first:last], b_sb[:].indirect(entries(idx2, first, last)), 1.0, 0.5, ALU.mult, ALU.add
+            )
+        nc.scalar.activation(e[:, 128:256], g[:, 128:256], ACT.Exp, bias=minus_half[:])
+        nc.scalar.activation(e_head, g[:, 0:128], ACT.Exp, bias=minus_half[:])
+
+        a_sb = sb.tile([P, T], F32)
+        for n in range(2):
+            first, last = 512 * n, 512 * (n + 1)
+            bank = scores(q_codes, q_scales, first, last, "a_bank%d" % n)
+            nc.vector.tensor_copy(out=a_sb[:, first:last], in_=bank[:])
+
+        def gather_a(dest, first, lam_wide):
+            nc.vector.tensor_tensor(dest, a_sb[:].indirect(entries(idx, first, first + 128)), lam_wide, ALU.mult)
+
+        gather_a(ag_head[:], 0, work[:, 0:128])
+        gather_a(work[:, 128:256], 256, lam_rows[:])
+
+        soft = sb.tile([P, 320], F32)
+        den = sb.tile([P, 384], F32)
+        pieces = (
+            (0, 128, e_head, soft[:, 0:128], work[:, 0:128]),
+            (128, 320, e[:, 128:320], soft[:, 128:320], den[:, 0:192]),
+            (320, 512, e[:, 320:512], work[:, 256:448], den[:, 192:384]),
+        )
+        for first, last, src, s, d in pieces:
+            nc.scalar.activation(s, src, ACT.Ln, bias=root_e[:], scale=ROOT_E)
+        for first, last, src, s, d in pieces:
+            nc.vector.scalar_tensor_tensor(d, s, CLAMP, g[:, first:last], ALU.min, ALU.max)
+        t = sb.tile([P, 384], F32)
+        for first in (0, 192):
+            nc.scalar.activation(t[:, first : first + 192], den[:, first : first + 192], ACT.Ln)
+
+        r_head = soft[:, 128:256]
+        nc.vector.reciprocal(r_head, work[:, 0:128])
+        nc.vector.tensor_tensor(f1[:].indirect(entries(idx, 0, 128)), ag_head[:], r_head, ALU.mult)
+
+        gather_a(work[:, 256:384], 384, lam_rows[:])
+        gather_a(work[:, 0:128], 128, lam_rows[:])
+        r_tail = sb.tile([P, 384], F32)
+        nc.scalar.activation(r_tail[:], t[:], ACT.Exp, scale=-1.0)
+        nc.vector.tensor_tensor(f1[:].indirect(entries(idx, 128, 512)), work[:, 0:384], r_tail[:], ALU.mult)
+
+        f2 = sb.tile([P, T], F32)
+        nc.vector.tensor_tensor(f2[:], f1[:], old_sb[:], ALU.add)
+
+
+        u = sb.tile([P, I], F32)
+        v = sb.tile([P, I], F32)
+        y = sb.tile([P, I], F32)
+        for first in (0, 256):
+            last = first + 256
+            nc.scalar.activation(u[:, first:last], f2[:].indirect(entries(idx3, first, last)), ACT.Copy)
+            nc.vector.tensor_copy(out=v[:, first:last], in_=f2[:].indirect(entries(idx4, first, last)))
+        for first in (0, 256):
+            last = first + 256
+            nc.vector.tensor_tensor(y[:, first:last], u[:, first:last], v[:, first:last], ALU.max)
+            nc.sync.dma_start(out[:, first:last], y[:, first:last])

@@ -61,19 +61,20 @@ def tile_attend_worthfor_lean_throughtwo_heads_kernel(
         nc.vector.memset(one[:], 1.0)
         root_e = sb.tile([P, 1], F32)
         nc.scalar.activation(root_e[:], one[:], ACT.Copy, scale=ROOT_E)
-        minus_half = sb.tile([P, 1], F32)
-        nc.vector.memset(minus_half[:], -0.5)
         f1 = sb.tile([P, T], F32)
         nc.vector.memset(f1[:], 0.0)
 
-        def interleave(raw, name):
+        def interleave(raw, name, split):
             grouped = sb.tile([P, Q, PACK], BF16, align_bytes=64, name=name + "_grouped")
-            nc.vector.tensor_copy(out=grouped[:], in_=raw[:].rearrange("p j q -> p q j"))
+            turned = raw[:].rearrange("p j q -> p q j")
+            nc.vector.tensor_copy(out=grouped[:, 0:split, :], in_=turned[:, 0:split, :])
+            if split < Q:
+                nc.scalar.copy(out=grouped[:, split:Q, :], in_=turned[:, split:Q, :])
             return grouped
 
         def quantise(grouped, name):
-            codes = sb.tile([P, Q], U32, align_bytes=64, name=name + "_codes", tag="codes")
-            scales = sb.tile([P, Q], U8, align_bytes=64, name=name + "_scales", tag="scales")
+            codes = sb.tile([P, Q], U32, align_bytes=64, name=name + "_codes")
+            scales = sb.tile([P, Q], U8, align_bytes=64, name=name + "_scales")
             nc.vector.quantize_mx(
                 out=codes[:].bitcast(FP8X4), scales=scales[:], in_=grouped[:].rearrange("p q j -> p (q j)")
             )
@@ -92,8 +93,8 @@ def tile_attend_worthfor_lean_throughtwo_heads_kernel(
             )
             return bank
 
-        q2_codes, q2_scales = quantise(interleave(q2_raw, "q2"), "q2")
-        q_grouped = interleave(q_raw, "q")
+        q2_codes, q2_scales = quantise(interleave(q2_raw, "q2", Q), "q2")
+        q_codes, q_scales = quantise(interleave(q_raw, "q", Q), "q")
 
 
         old_sb = sb.tile([P, T], F32, tag="q2_then_old")
@@ -104,68 +105,59 @@ def tile_attend_worthfor_lean_throughtwo_heads_kernel(
         nc.sync.dma_start(idx4[:], offs4)
 
         b_sb = sb.tile([P, T], F32)
-        for n in range(4):
-            first, last = 256 * n, 256 * (n + 1)
+        for n, (first, last) in enumerate(((0, 512), (512, 768), (768, 896), (896, 1024))):
             bank = scores(q2_codes, q2_scales, first, last, "b_bank%d" % n)
             if n % 2:
                 nc.vector.tensor_copy(out=b_sb[:, first:last], in_=bank[:])
             else:
                 nc.scalar.copy(out=b_sb[:, first:last], in_=bank[:])
 
-        q_codes, q_scales = quantise(q_grouped, "q")
         e = sb.tile([P, I], F32)
-        g = sb.tile([P, I], F32)
-        work = sb.tile([P, 448], F32)
-        ag_head = sb.tile([P, 128], F32)
+        picked = sb.tile([P, 128 + I], F32)
+        g = picked[:, 128:]
+        den = sb.tile([P, I], F32)
         lam_rows = sb.tile([P, 128], F32)
-        nc.scalar.copy(out=lam_rows[:], in_=lam_col[:].to_broadcast([P, 128]))
-        nc.scalar.copy(out=work[:, 0:128], in_=lam_col[:].to_broadcast([P, 128]))
-        e_head = work[:, 256:384]
-        nc.scalar.activation(e[:, 256:512], b_sb[:].indirect(entries(idx2, 256, 512)), ACT.Exp)
-        for first in (0, 256):
-            last = first + 256
-            nc.vector.tensor_scalar(
-                g[:, first:last], b_sb[:].indirect(entries(idx2, first, last)), 1.0, 0.5, ALU.mult, ALU.add
-            )
-        nc.scalar.activation(e[:, 128:256], g[:, 128:256], ACT.Exp, bias=minus_half[:])
-        nc.scalar.activation(e_head, g[:, 0:128], ACT.Exp, bias=minus_half[:])
+        nc.gpsimd.tensor_scalar(den[:, 160:416], lam_col[:].to_broadcast([P, 256]), 1.0, 0.0, ALU.mult, ALU.add)
+        nc.gpsimd.tensor_scalar(lam_rows[:], lam_col[:].to_broadcast([P, 128]), 1.0, 0.0, ALU.mult, ALU.add)
+        nc.scalar.activation(e[:], b_sb[:].indirect(idx2[:]), ACT.Exp)
 
         a_sb = sb.tile([P, T], F32)
         for n in range(2):
             first, last = 512 * n, 512 * (n + 1)
             bank = scores(q_codes, q_scales, first, last, "a_bank%d" % n)
             nc.vector.tensor_copy(out=a_sb[:, first:last], in_=bank[:])
+        nc.vector.tensor_scalar(g, b_sb[:].indirect(idx2[:]), 1.0, 0.5, ALU.mult, ALU.add)
 
         def gather_a(dest, first, lam_wide):
             nc.vector.tensor_tensor(dest, a_sb[:].indirect(entries(idx, first, first + 128)), lam_wide, ALU.mult)
 
-        gather_a(ag_head[:], 0, work[:, 0:128])
-        gather_a(work[:, 128:256], 256, lam_rows[:])
+        ag_head = sb.tile([P, 128], F32)
+        gather_a(ag_head[:], 0, den[:, 160:288])
+        gather_a(picked[:, 0:128], 128, den[:, 288:416])
 
-        soft = sb.tile([P, 320], F32)
-        den = sb.tile([P, 384], F32)
+        soft = sb.tile([P, I], F32)
         pieces = (
-            (0, 128, e_head, soft[:, 0:128], work[:, 0:128]),
-            (128, 320, e[:, 128:320], soft[:, 128:320], den[:, 0:192]),
-            (320, 512, e[:, 320:512], work[:, 256:448], den[:, 192:384]),
+            (128, 320, soft[:, 0:192], den[:, 0:192]),
+            (320, 512, soft[:, 192:384], den[:, 192:384]),
+            (0, 128, soft[:, 384:512], den[:, 384:512]),
         )
-        for first, last, src, s, d in pieces:
-            nc.scalar.activation(s, src, ACT.Ln, bias=root_e[:], scale=ROOT_E)
-        for first, last, src, s, d in pieces:
+        for first, last, s, d in pieces:
+            nc.scalar.activation(s, e[:, first:last], ACT.Ln, bias=root_e[:], scale=ROOT_E)
+        for first, last, s, d in pieces:
             nc.vector.scalar_tensor_tensor(d, s, CLAMP, g[:, first:last], ALU.min, ALU.max)
         t = sb.tile([P, 384], F32)
         for first in (0, 192):
             nc.scalar.activation(t[:, first : first + 192], den[:, first : first + 192], ACT.Ln)
 
-        r_head = soft[:, 128:256]
-        nc.vector.reciprocal(r_head, work[:, 0:128])
-        nc.vector.tensor_tensor(f1[:].indirect(entries(idx, 0, 128)), ag_head[:], r_head, ALU.mult)
+        r_head = sb.tile([P, 128], F32)
+        nc.vector.reciprocal(r_head[:], den[:, 384:512])
+        nc.vector.tensor_tensor(f1[:].indirect(entries(idx, 0, 128)), ag_head[:], r_head[:], ALU.mult)
 
-        gather_a(work[:, 256:384], 384, lam_rows[:])
-        gather_a(work[:, 0:128], 128, lam_rows[:])
+        gather_a(picked[:, 256:384], 384, lam_rows[:])
+        gather_a(picked[:, 128:256], 256, lam_rows[:])
         r_tail = sb.tile([P, 384], F32)
         nc.scalar.activation(r_tail[:], t[:], ACT.Exp, scale=-1.0)
-        nc.vector.tensor_tensor(f1[:].indirect(entries(idx, 128, 512)), work[:, 0:384], r_tail[:], ALU.mult)
+        nc.vector.tensor_tensor(f1[:].indirect(entries(idx, 128, 512)), picked[:, 0:384], r_tail[:], ALU.mult)
 
         f2 = sb.tile([P, T], F32)
         nc.vector.tensor_tensor(f2[:], f1[:], old_sb[:], ALU.add)

@@ -42,18 +42,19 @@ def tile_attend_worthfor_lean_throughtwo_heads_kernel(
         key_scales = sb.tile([P, T], U8, align_bytes=64)
 
         for quad in range(4):
-            nc.scalar.dma_start(
+            queue = nc.scalar if quad % 2 else nc.sync
+            queue.dma_start(
                 key_scales[32 * quad : 32 * quad + 4, :].bitcast(I32),
                 keys_scales[0, 4 * quad : 4 * quad + 4, :].bitcast(I32),
             )
+        lam_col = sb.tile([P, 1], F32)
+        nc.scalar.dma_start(lam_col[:], lam)
         key_words = sb.tile([P, 2 * T], U8, align_bytes=64)
         nc.sync.dma_start(key_words[:].bitcast(I32), keys_words[0].bitcast(I32))
         q_raw = sb.tile([P, PACK, Q], F32)
         nc.sync.dma_start(q_raw[:], query.rearrange("(p j) q -> p j q", j=PACK))
         idx2 = lists.tile([P, I // 16], U16)
         nc.sync.dma_start(idx2[:], offs2)
-        lam_col = sb.tile([P, 1], F32)
-        nc.gpsimd.dma_start(lam_col[:], lam)
         idx = lists.tile([P, I // 16], U16)
         nc.sync.dma_start(idx[:], offs)
 
@@ -64,6 +65,11 @@ def tile_attend_worthfor_lean_throughtwo_heads_kernel(
         f1 = sb.tile([P, T], F32)
         nc.vector.memset(f1[:], 0.0)
 
+        den = sb.tile([P, I], F32)
+        lam_rows = sb.tile([P, 128], F32)
+        nc.scalar.copy(out=den[:, 160:416], in_=lam_col[:].to_broadcast([P, 256]))
+        nc.scalar.copy(out=lam_rows[:], in_=lam_col[:].to_broadcast([P, 128]))
+
         def interleave(raw, name, split):
             grouped = sb.tile([P, Q, PACK], BF16, align_bytes=64, name=name + "_grouped")
             turned = raw[:].rearrange("p j q -> p q j")
@@ -73,8 +79,8 @@ def tile_attend_worthfor_lean_throughtwo_heads_kernel(
             return grouped
 
         def quantise(grouped, name):
-            codes = sb.tile([P, Q], U32, align_bytes=64, name=name + "_codes")
-            scales = sb.tile([P, Q], U8, align_bytes=64, name=name + "_scales")
+            codes = sb.tile([P, Q], U32, align_bytes=64, name=name + "_codes", tag="codes")
+            scales = sb.tile([P, Q], U8, align_bytes=64, name=name + "_scales", tag="scales")
             nc.vector.quantize_mx(
                 out=codes[:].bitcast(FP8X4), scales=scales[:], in_=grouped[:].rearrange("p q j -> p (q j)")
             )
@@ -94,7 +100,7 @@ def tile_attend_worthfor_lean_throughtwo_heads_kernel(
             return bank
 
         q2_codes, q2_scales = quantise(interleave(q2_raw, "q2", Q), "q2")
-        q_codes, q_scales = quantise(interleave(q_raw, "q", Q), "q")
+        q_grouped = interleave(q_raw, "q", Q)
 
 
         old_sb = sb.tile([P, T], F32, tag="q2_then_old")
@@ -112,13 +118,10 @@ def tile_attend_worthfor_lean_throughtwo_heads_kernel(
             else:
                 nc.scalar.copy(out=b_sb[:, first:last], in_=bank[:])
 
+        q_codes, q_scales = quantise(q_grouped, "q")
         e = sb.tile([P, I], F32)
         picked = sb.tile([P, 128 + I], F32)
         g = picked[:, 128:]
-        den = sb.tile([P, I], F32)
-        lam_rows = sb.tile([P, 128], F32)
-        nc.gpsimd.tensor_scalar(den[:, 160:416], lam_col[:].to_broadcast([P, 256]), 1.0, 0.0, ALU.mult, ALU.add)
-        nc.gpsimd.tensor_scalar(lam_rows[:], lam_col[:].to_broadcast([P, 128]), 1.0, 0.0, ALU.mult, ALU.add)
         nc.scalar.activation(e[:], b_sb[:].indirect(idx2[:]), ACT.Exp)
 
         a_sb = sb.tile([P, T], F32)
@@ -170,7 +173,6 @@ def tile_attend_worthfor_lean_throughtwo_heads_kernel(
             last = first + 256
             nc.scalar.activation(u[:, first:last], f2[:].indirect(entries(idx3, first, last)), ACT.Copy)
             nc.vector.tensor_copy(out=v[:, first:last], in_=f2[:].indirect(entries(idx4, first, last)))
-        for first in (0, 256):
-            last = first + 256
+        for first, last, queue in ((0, 256, nc.sync), (256, 384, nc.scalar), (384, 512, nc.sync)):
             nc.vector.tensor_tensor(y[:, first:last], u[:, first:last], v[:, first:last], ALU.max)
-            nc.sync.dma_start(out[:, first:last], y[:, first:last])
+            queue.dma_start(out[:, first:last], y[:, first:last])

@@ -173,6 +173,7 @@ def tile_attend_worthfor_lean_throughtwo_heads_kernel(
             last = first + 256
             nc.scalar.activation(u[:, first:last], f2[:].indirect(entries(idx3, first, last)), ACT.Copy)
             nc.vector.tensor_copy(out=v[:, first:last], in_=f2[:].indirect(entries(idx4, first, last)))
-        for first, last, queue in ((0, 256, nc.sync), (256, 384, nc.scalar), (384, 512, nc.sync)):
+        for first in (0, 256):
+            last = first + 256
             nc.vector.tensor_tensor(y[:, first:last], u[:, first:last], v[:, first:last], ALU.max)
-            queue.dma_start(out[:, first:last], y[:, first:last])
+            nc.sync.dma_start(out[:, first:last], y[:, first:last])

import math
from contextlib import ExitStack

import concourse.mybir as mybir


D, T, I, Q = 512, 1024, 512, 128
FLOPS = 2 * 2 * D * T * Q

F32 = mybir.dt.float32
BF16 = mybir.dt.bfloat16
I32 = mybir.dt.int32
U32 = mybir.dt.uint32
U16 = mybir.dt.uint16
U8 = mybir.dt.uint8
FP8X4 = mybir.dt.float8_e4m3fn_x4
FP4X4 = mybir.dt.float4_e2m1fn_x4
ALU = mybir.AluOpType
ACT = mybir.ActivationFunctionType

P = 128
PACK = 4
CLAMP = 41.5
ROOT_E = math.exp(0.5)


def entries(offsets, first, last):
    return offsets[:, first // 16 : last // 16]


def tile_attend_worthfor_lean_throughtwo_heads_kernel(
    tc, query, query2, keys_words, keys_scales, lam, old, offs, offs2, offs3, offs4, out
):
    nc = tc.nc
    with ExitStack() as ctx:
        lists = ctx.enter_context(tc.tile_pool(name="lists", bufs=1))
        sb = ctx.enter_context(tc.tile_pool(name="sb", bufs=1))
        psum = ctx.enter_context(tc.psum_pool(name="psum", bufs=1))

        q2_raw = sb.tile([P, PACK, Q], F32, tag="q2_then_old")
        nc.sync.dma_start(q2_raw[:], query2.rearrange("(p j) q -> p j q", j=PACK))
        key_scales = sb.tile([P, T], U8, align_bytes=64)

        for quad in range(4):
            queue = nc.scalar if quad % 2 else nc.sync
            queue.dma_start(
                key_scales[32 * quad : 32 * quad + 4, :].bitcast(I32),
                keys_scales[0, 4 * quad : 4 * quad + 4, :].bitcast(I32),
            )
        lam_col = sb.tile([P, 1], F32)
        nc.scalar.dma_start(lam_col[:], lam)
        key_words = sb.tile([P, 2 * T], U8, align_bytes=64)
        nc.sync.dma_start(key_words[:].bitcast(I32), keys_words[0].bitcast(I32))
        q_raw = sb.tile([P, PACK, Q], F32)
        nc.sync.dma_start(q_raw[:], query.rearrange("(p j) q -> p j q", j=PACK))
        idx2 = lists.tile([P, I // 16], U16)
        nc.sync.dma_start(idx2[:], offs2)
        idx = lists.tile([P, I // 16], U16)
        nc.sync.dma_start(idx[:], offs)

        one = sb.tile([P, 1], F32)
        nc.vector.memset(one[:], 1.0)
        root_e = sb.tile([P, 1], F32)
        nc.scalar.activation(root_e[:], one[:], ACT.Copy, scale=ROOT_E)
        f1 = sb.tile([P, T], F32)
        nc.vector.memset(f1[:], 0.0)

        den = sb.tile([P, I], F32)
        lam_rows = sb.tile([P, 128], F32)
        nc.scalar.copy(out=den[:, 160:416], in_=lam_col[:].to_broadcast([P, 256]))
        nc.scalar.copy(out=lam_rows[:], in_=lam_col[:].to_broadcast([P, 128]))

        def interleave(raw, name, split):
            grouped = sb.tile([P, Q, PACK], BF16, align_bytes=64, name=name + "_grouped")
            turned = raw[:].rearrange("p j q -> p q j")
            nc.vector.tensor_copy(out=grouped[:, 0:split, :], in_=turned[:, 0:split, :])
            if split < Q:
                nc.scalar.copy(out=grouped[:, split:Q, :], in_=turned[:, split:Q, :])
            return grouped

        def quantise(grouped, name):
            codes = sb.tile([P, Q], U32, align_bytes=64, name=name + "_codes", tag="codes")
            scales = sb.tile([P, Q], U8, align_bytes=64, name=name + "_scales", tag="scales")
            nc.vector.quantize_mx(
                out=codes[:].bitcast(FP8X4), scales=scales[:], in_=grouped[:].rearrange("p q j -> p (q j)")
            )
            return codes, scales

        def scores(codes, scales, first, last, name):
            bank = psum.tile([P, last - first], F32, name=name)
            nc.tensor.matmul_mx(
                out=bank[:],
                lhsT=codes[:].bitcast(FP8X4),
                lhsT_scale=scales[:],
                rhs=key_words[:, 2 * first : 2 * last].bitcast(FP4X4),
                rhs_scale=key_scales[:, first:last],
                start=True,
                stop=True,
            )
            return bank

        q2_codes, q2_scales = quantise(interleave(q2_raw, "q2", Q), "q2")
        q_grouped = interleave(q_raw, "q", Q)


        old_sb = sb.tile([P, T], F32, tag="q2_then_old")
        nc.sync.dma_start(old_sb[:], old)
        idx3 = lists.tile([P, I // 16], U16)
        nc.sync.dma_start(idx3[:], offs3)
        idx4 = lists.tile([P, I // 16], U16)
        nc.sync.dma_start(idx4[:], offs4)

        b_sb = sb.tile([P, T], F32)
        for n, (first, last) in enumerate(((0, 512), (512, 768), (768, 896), (896, 1024))):
            bank = scores(q2_codes, q2_scales, first, last, "b_bank%d" % n)
            if n % 2:
                nc.vector.tensor_copy(out=b_sb[:, first:last], in_=bank[:])
            else:
                nc.scalar.copy(out=b_sb[:, first:last], in_=bank[:])

        q_codes, q_scales = quantise(q_grouped, "q")
        e = sb.tile([P, I], F32)
        picked = sb.tile([P, 128 + I], F32)
        g = picked[:, 128:]
        nc.scalar.activation(e[:], b_sb[:].indirect(idx2[:]), ACT.Exp)

        a_sb = sb.tile([P, T], F32)
        for n in range(2):
            first, last = 512 * n, 512 * (n + 1)
            bank = scores(q_codes, q_scales, first, last, "a_bank%d" % n)
            nc.vector.tensor_copy(out=a_sb[:, first:last], in_=bank[:])
        nc.vector.tensor_scalar(g, b_sb[:].indirect(idx2[:]), 1.0, 0.5, ALU.mult, ALU.add)

        def gather_a(dest, first, lam_wide):
            nc.vector.tensor_tensor(dest, a_sb[:].indirect(entries(idx, first, first + 128)), lam_wide, ALU.mult)

        ag_head = sb.tile([P, 128], F32)
        gather_a(ag_head[:], 0, den[:, 160:288])
        gather_a(picked[:, 0:128], 128, den[:, 288:416])

        soft = sb.tile([P, I], F32)
        pieces = (
            (128, 320, soft[:, 0:192], den[:, 0:192]),
            (320, 512, soft[:, 192:384], den[:, 192:384]),
            (0, 128, soft[:, 384:512], den[:, 384:512]),
        )
        for first, last, s, d in pieces:
            nc.scalar.activation(s, e[:, first:last], ACT.Ln, bias=root_e[:], scale=ROOT_E)
        for first, last, s, d in pieces:
            nc.vector.scalar_tensor_tensor(d, s, CLAMP, g[:, first:last], ALU.min, ALU.max)
        t = sb.tile([P, 384], F32)
        for first in (0, 192):
            nc.scalar.activation(t[:, first : first + 192], den[:, first : first + 192], ACT.Ln)

        r_head = sb.tile([P, 128], F32)
        nc.vector.reciprocal(r_head[:], den[:, 384:512])
        nc.vector.tensor_tensor(f1[:].indirect(entries(idx, 0, 128)), ag_head[:], r_head[:], ALU.mult)

        gather_a(picked[:, 256:384], 384, lam_rows[:])
        gather_a(picked[:, 128:256], 256, lam_rows[:])
        r_tail = sb.tile([P, 384], F32)
        nc.scalar.activation(r_tail[:], t[:], ACT.Exp, scale=-1.0)
        nc.vector.tensor_tensor(f1[:].indirect(entries(idx, 128, 512)), picked[:, 0:384], r_tail[:], ALU.mult)

        f2 = sb.tile([P, T], F32)
        nc.vector.tensor_tensor(f2[:], f1[:], old_sb[:], ALU.add)


        u = sb.tile([P, I], F32)
        v = sb.tile([P, I], F32)
        y = sb.tile([P, I], F32)
        for first in (0, 256):
            last = first + 256
            nc.scalar.activation(u[:, first:last], f2[:].indirect(entries(idx3, first, last)), ACT.Copy)
            nc.vector.tensor_copy(out=v[:, first:last], in_=f2[:].indirect(entries(idx4, first, last)))
        for first in (0, 256):
            last = first + 256
            nc.vector.tensor_tensor(y[:, first:last], u[:, first:last], v[:, first:last], ALU.max)
            nc.sync.dma_start(out[:, first:last], y[:, first:last])
